import numpy as np
import ml_dtypes


def mxq(x, axis, fmt="e4m3"):
    dtype, down = {"e4m3": (ml_dtypes.float8_e4m3fn, 7), "e5m2": (ml_dtypes.float8_e5m2, 14)}[fmt]
    v = np.moveaxis(np.asarray(x, np.float32).astype(ml_dtypes.bfloat16).astype(np.float64), axis, -1)
    blocks = v.reshape(v.shape[:-1] + (-1, 32))
    amax = np.abs(blocks).max(-1, keepdims=True)
    byte = np.maximum(np.where(amax > 0, np.frexp(amax)[1] - 1 + 127, 0) - down, 1)
    scale = np.exp2(byte - 127.0)
    codes = (blocks / scale).astype(np.float32).astype(dtype).astype(np.float64)
    return np.moveaxis((codes * scale).reshape(v.shape), -1, axis)


WIDE = False


def mx_kscale(k):
    if not WIDE:
        return np.ones(k)
    levels = np.array([10, -10, 5, -5, 0])
    if k % 512:
        return np.exp2(np.random.permutation(np.resize(levels, k // 32))).repeat(32)
    a = np.empty((k // 512, 16))
    for p in range(k // 512):
        a[p, :8] = np.random.permutation(np.resize(levels, 8))
        for g in range(8):
            far = levels[np.abs(levels - a[p, g]) >= 10]
            a[p, g + 8] = far[np.random.randint(len(far))]
    return np.exp2(a.ravel()).repeat(32)


def f64(x):
    return np.asarray(x).astype(np.float64)


def striped8(idx):
    return np.asarray(idx).reshape(8, -1, 16).transpose(0, 2, 1).reshape(128, -1).astype(np.uint16)


def unstriped8(offs):
    return offs.reshape(8, 16, -1).transpose(0, 2, 1).reshape(8, -1).astype(np.int64)


def pick8(x, idx, run):
    r = np.arange(len(x))
    return x[r[:, None], idx[r % (8 * run) // run]]


E2M1 = np.array([0.0, 0.5, 1.0, 1.5, 2.0, 3.0, 4.0, 6.0, -0.0, -0.5, -1.0, -1.5, -2.0, -3.0, -4.0, -6.0])


def pack_weight(w, fmt):
    k, n = w.shape
    w = f64(np.asarray(w, np.float32).astype(ml_dtypes.bfloat16)).reshape(k // 32, 32, n)
    amax = np.abs(w).max(1)
    if fmt == "e4m3":
        byte = np.frexp(amax)[1] - 1 + 127 - 7
    else:
        mant, ex = np.frexp(amax / 6.0)
        byte = np.where(mant > 0.5, ex, ex - 1) + 127
    byte = np.clip(np.where(amax > 0, byte, 1), 1, 254)
    scaled = (w * np.exp2(127.0 - byte)[:, None, :]).reshape(k, n).astype(np.float32)
    by_word = np.ascontiguousarray(scaled.reshape(k // 512, 128, 4, n).transpose(0, 1, 3, 2))
    if fmt == "e4m3":
        words = by_word.astype(ml_dtypes.float8_e4m3fn).view(np.uint8)
    else:
        c = by_word.astype(ml_dtypes.float4_e2m1fn).view(np.uint8) & 0xF
        words = (c[..., 0::2] | (c[..., 1::2] << 4)).reshape(k // 512, 128, 2 * n)
    return np.ascontiguousarray(words), np.ascontiguousarray(byte.astype(np.uint8).reshape(k // 512, 16, n))


def unpack_weight(words, scales, fmt):
    g, _, n = scales.shape
    words = np.ascontiguousarray(words).reshape(g, 128, n, -1)
    if fmt == "e4m3":
        vals = words.view(ml_dtypes.float8_e4m3fn).astype(np.float64)
    else:
        nib = np.empty((g, 128, n, 4), np.uint8)
        nib[..., 0::2] = words & 0xF
        nib[..., 1::2] = words >> 4
        vals = E2M1[nib]
    vals = vals * np.repeat(np.exp2(scales.astype(np.float64) - 127.0), 8, axis=1)[..., None]
    return vals.transpose(0, 1, 3, 2).reshape(g * 512, n)


D, T, U, X, I, Q, E = 512, 1024, 1024, 1024, 512, 512, 256


def setup_inputs():
    n = np.random.standard_normal
    idx = np.stack([np.random.permutation(T)[:I] for _ in range(8)])
    idx2 = np.stack([np.random.permutation(U)[:I] for _ in range(8)])
    idx3 = np.stack([np.random.permutation(X)[:I] for _ in range(8)])
    idx4 = np.stack([np.random.permutation(X)[:I] for _ in range(8)])
    fd = mx_kscale(D)
    fq = mx_kscale(Q)
    keysp = pack_weight(n((D, T)) / fd[:, None], "e4m3")
    notesp = pack_weight(n((D, U)) / fd[:, None], "e2m1")
    usersp = pack_weight(n((D, X)) / fd[:, None], "e2m1")
    mixp = pack_weight(n((Q, E)) * 1.0 / np.sqrt(Q) / fq[:, None], "e2m1")
    return {
        "query": (n((D, Q)) * 1.0 / np.sqrt(D) * fd[:, None]).astype(np.float32),
        "query2": (n((D, Q)) * 1.0 / np.sqrt(D) * fd[:, None]).astype(np.float32),
        "keys_words": keysp[0],
        "keys_scales": keysp[1],
        "notes_words": notesp[0],
        "notes_scales": notesp[1],
        "users_words": usersp[0],
        "users_scales": usersp[1],
        "lam": (np.random.uniform(0.5, 1.5, (Q, 1))).astype(np.float32),
        "rowf": (np.random.uniform(0.5, 2.0, (Q, 1)) * fq[:, None]).astype(np.float32),
        "mix_words": mixp[0],
        "mix_scales": mixp[1],
        "offs": striped8(idx),
        "offs2": striped8(idx2),
        "offs3": striped8(idx3),
        "offs4": striped8(idx4),
    }


def reference(query, query2, keys_words, keys_scales, notes_words, notes_scales, users_words, users_scales, lam, rowf, mix_words, mix_scales, offs, offs2, offs3, offs4):
    idx = unstriped8(offs)
    idx2 = unstriped8(offs2)
    idx3 = unstriped8(offs3)
    idx4 = unstriped8(offs4)
    keysu = unpack_weight(keys_words, keys_scales, "e4m3")
    notesu = unpack_weight(notes_words, notes_scales, "e2m1")
    usersu = unpack_weight(users_words, users_scales, "e2m1")
    mixu = unpack_weight(mix_words, mix_scales, "e2m1")
    queryq = mxq(f64(query), 0, "e4m3")
    a = queryq.T @ keysu
    b = queryq.T @ notesu
    query2q = mxq(f64(query2), 0, "e4m3")
    c0 = query2q.T @ usersu
    r = pick8(a, idx, 64) - pick8(b, idx2, 64)
    f1 = np.zeros((Q, X))
    f1[np.arange(Q)[:, None], idx3[np.arange(Q) % 512 // 64]] = r
    cc = c0 + f1 * f64(lam)
    g = pick8(cc, idx4, 64) - r
    gw = g * f64(rowf)
    gwq = mxq(gw, 0, "e4m3")
    y = mixu.T @ gwq
    return y

@@ -1,0 +1,236 @@
+from contextlib import ExitStack
+
+import concourse.mybir as mybir
+
+F32 = mybir.dt.float32
+BF16 = mybir.dt.bfloat16
+I32 = mybir.dt.int32
+U32 = mybir.dt.uint32
+U16 = mybir.dt.uint16
+U8 = mybir.dt.uint8
+FP8X4 = mybir.dt.float8_e4m3fn_x4
+FP4X4 = mybir.dt.float4_e2m1fn_x4
+MULT = mybir.AluOpType.mult
+ADD = mybir.AluOpType.add
+SUB = mybir.AluOpType.subtract
+COPY = mybir.ActivationFunctionType.Copy
+
+P = 128
+PACK = 4
+Q = 512
+COLS = 1024
+SLOTS = 512
+E = 256
+BANK = 512
+HALF = SLOTS // 2
+LIST_COLS = SLOTS // 16
+
+FLOPS = 2 * 512 * 512 * 3 * 1024 + 2 * 512 * 256 * 512
+
+
+def tile_attend_tugged_threeq_mixed_kernel(
+    tc, query, query2, keys_words, keys_scales, notes_words, notes_scales, users_words, users_scales,
+    lam, rowf, mix_words, mix_scales, offs, offs2, offs3, offs4, out,
+):
+    nc = tc.nc
+    with ExitStack() as ctx:
+        keep = ctx.enter_context(tc.tile_pool(name="keep", bufs=1))
+        psum = ctx.enter_context(tc.psum_pool(name="psum", bufs=1))
+
+        def load_query_half(src, h, name):
+            raw = keep.tile([P, PACK, Q // 2], F32, name=name)
+            rows = src.rearrange("(p t) q -> p t q", t=PACK)
+            nc.sync.dma_start(out=raw[:], in_=rows[:, :, h * (Q // 2):(h + 1) * (Q // 2)])
+            return raw
+
+        def load_scales(src, width, name):
+            plane = keep.tile([P, width], U8, name=name, align_bytes=64)
+            rows = src[0].bitcast(I32)
+            for r in range(4):
+                nc.sync.dma_start(out=plane[r:P:32, :].bitcast(I32), in_=rows[r:16:4, :])
+            return plane
+
+        def load_fp4_words(src, width, name):
+            words = keep.tile([P, 2 * width], U8, name=name, align_bytes=64)
+            nc.sync.dma_start(out=words[:].bitcast(I32), in_=src[0].bitcast(I32))
+            return words
+
+        def load_list(src, name):
+            lst = keep.tile([P, LIST_COLS], U16, name=name)
+            nc.sync.dma_start(out=lst[:], in_=src)
+            return lst
+
+        def load_row_factor(src, name):
+            col = keep.tile([P, PACK], F32, name=name)
+            nc.sync.dma_start(out=col[:], in_=src.rearrange("(p j) o -> p (j o)", j=PACK))
+            return col
+
+        q_raw0 = load_query_half(query, 0, "q_raw0")
+        q_raw1 = load_query_half(query, 1, "q_raw1")
+        notes_s = load_scales(notes_scales, COLS, "notes_s")
+        notes_w = load_fp4_words(notes_words, COLS, "notes_w")
+        keys_w = keep.tile([P, COLS], U32, name="keys_w", align_bytes=64)
+        nc.sync.dma_start(out=keys_w[:].bitcast(I32), in_=keys_words[0].rearrange("p n t -> p (n t)").bitcast(I32))
+        keys_s = load_scales(keys_scales, COLS, "keys_s")
+        q2_raw0 = load_query_half(query2, 0, "q2_raw0")
+        q2_raw1 = load_query_half(query2, 1, "q2_raw1")
+        note_list = load_list(offs2, "note_list")
+        token_list = load_list(offs, "token_list")
+        put_list = load_list(offs3, "put_list")
+        users_w = load_fp4_words(users_words, COLS, "users_w")
+        users_s = load_scales(users_scales, COLS, "users_s")
+        lam_c = load_row_factor(lam, "lam_c")
+        user_list = load_list(offs4, "user_list")
+        rowf_c = load_row_factor(rowf, "rowf_c")
+        mix_w = load_fp4_words(mix_words, E, "mix_w")
+        mix_s = load_scales(mix_scales, E, "mix_s")
+
+        f1 = keep.tile([P, COLS], F32, name="f1")
+        nc.gpsimd.memset(f1[:], 0.0)
+
+        def dealt(tile, h):
+            return tile[:, :, h * 64:(h + 1) * 64, :].rearrange("p j m t -> p m t j")
+
+        def as_loaded(raw):
+            return raw[:].rearrange("p t (m j) -> p m t j", j=PACK)
+
+        q_bf = keep.tile([P, PACK, P, PACK], BF16, name="q_bf", align_bytes=64)
+        nc.scalar.copy(dealt(q_bf, 0), as_loaded(q_raw0))
+        nc.vector.tensor_copy(dealt(q_bf, 1), as_loaded(q_raw1))
+        q_codes = keep.tile([P, Q], U32, name="q_codes", align_bytes=64)
+        q_scales = keep.tile([P, Q], U8, name="q_scales", align_bytes=64)
+        for j0, j1 in ((0, 1), (1, 2), (2, 4)):
+            nc.vector.quantize_mx(
+                out=q_codes[:, j0 * P:j1 * P].bitcast(FP8X4),
+                scales=q_scales[:, j0 * P:j1 * P],
+                in_=q_bf[:, j0:j1, :, :].rearrange("p j m t -> p (j m t)"),
+            )
+
+        q2_bf = keep.tile([P, PACK, P, PACK], BF16, name="q2_bf", tag="q2_bf", align_bytes=64)
+        nc.gpsimd.tensor_scalar(dealt(q2_bf, 0), as_loaded(q2_raw0), 1.0, 0.0, MULT, ADD)
+        nc.gpsimd.tensor_scalar(dealt(q2_bf, 1), as_loaded(q2_raw1), 1.0, 0.0, MULT, ADD)
+        q2_codes = keep.tile([P, Q], U32, name="q2_codes", align_bytes=64)
+        q2_scales = keep.tile([P, Q], U8, name="q2_scales", align_bytes=64)
+
+        def score(codes, scales, j, moving, moving_scales, pair, n):
+            bank = psum.tile([P, BANK], F32, name="bank%d%d" % (pair, n), tag="bank%d%d" % (pair, n))
+            nc.tensor.matmul_mx(
+                out=bank[:], lhsT=codes[:, j * P:(j + 1) * P].bitcast(FP8X4), lhsT_scale=scales[:, j * P:(j + 1) * P],
+                rhs=moving, rhs_scale=moving_scales[:, n * BANK:(n + 1) * BANK], start=True, stop=True,
+            )
+            return bank
+
+        def fp4_cols(words, n, width):
+            return words[:, 2 * n * width:2 * (n + 1) * width].bitcast(FP4X4)
+
+        def half_list(lst, h):
+            return lst[:, h * (LIST_COLS // 2):(h + 1) * (LIST_COLS // 2)]
+
+        def half(tile, h):
+            return tile[:, h * HALF:(h + 1) * HALF]
+
+        def note_scores(j, pair):
+            win = keep.tile([P, COLS], F32, name="b_win", tag="b_win", bufs=2)
+            for n in range(2):
+                bank = score(q_codes, q_scales, j, fp4_cols(notes_w, n, BANK), notes_s, pair, n)
+                nc.scalar.copy(win[:, n * BANK:(n + 1) * BANK], bank[:])
+            return win
+
+        def token_scores(j, pair, win, copy):
+            for n in range(2):
+                bank = score(q_codes, q_scales, j, keys_w[:, n * BANK:(n + 1) * BANK].bitcast(FP8X4), keys_s, pair, n)
+                copy(win[:, n * BANK:(n + 1) * BANK], bank[:])
+
+        def lead_of(j, b_win, a_pair):
+            a_win = keep.tile([P, COLS], F32, name="a_win", tag="a_win")
+            token_scores(j, a_pair, a_win, nc.scalar.copy)
+            b_got = keep.tile([P, SLOTS], F32, name="b_got", tag="b_got", bufs=2)
+            a_got = keep.tile([P, SLOTS], F32, name="a_got", tag="a_got", bufs=2)
+            lead = keep.tile([P, SLOTS], F32, name="lead%d" % j)
+            nc.scalar.activation(b_got[:], b_win[:].indirect(note_list[:]), COPY)
+            nc.scalar.activation(a_got[:], a_win[:].indirect(token_list[:]), COPY)
+            nc.gpsimd.tensor_tensor(lead[:], a_got[:], b_got[:], SUB)
+            return lead
+
+        def user_scores(j, pair):
+            cc_win = keep.tile([P, COLS], F32, name="cc%d" % j)
+            for n in range(2):
+                bank = score(q2_codes, q2_scales, j, fp4_cols(users_w, n, BANK), users_s, pair, n)
+                cols = slice(n * BANK, (n + 1) * BANK)
+                nc.vector.scalar_tensor_tensor(cc_win[:, cols], f1[:, cols], lam_c[:, j:j + 1], bank[:], MULT, ADD)
+            return cc_win
+
+        b_win0 = note_scores(0, 0)
+        a_win0 = keep.tile([P, COLS], F32, name="a_win0")
+        token_scores(0, 1, a_win0, nc.vector.tensor_copy)
+        b_got0 = keep.tile([P, SLOTS], F32, name="b_got", tag="b_got", bufs=2)
+        for h in range(2):
+            nc.scalar.activation(half(b_got0, h), b_win0[:].indirect(half_list(note_list, h)), COPY)
+        lead0 = []
+        for h in range(2):
+            if h == 0:
+                part = keep.tile([P, HALF], F32, name="lead0_first")
+            else:
+                nc.vector.quantize_mx(
+                    out=q2_codes[:].bitcast(FP8X4), scales=q2_scales[:], in_=q2_bf[:].rearrange("p j m t -> p (j m t)"),
+                )
+                part = keep.tile([P, HALF], F32, name="lead0_second", tag="q2_bf", align_bytes=64)
+            nc.vector.tensor_tensor(part[:], a_win0[:].indirect(half_list(token_list, h)), half(b_got0, h), SUB)
+            nc.vector.tensor_copy(f1[:].indirect(half_list(put_list, h)), part[:])
+            lead0.append(part)
+
+        leads = [None, lead_of(1, note_scores(1, 2), 0), lead_of(2, note_scores(2, 1), 2)]
+        b_win3 = note_scores(3, 0)
+        cc_wins = [user_scores(0, 3)]
+        leads.append(lead_of(3, b_win3, 3))
+        for j in range(1, PACK):
+            nc.vector.tensor_copy(f1[:].indirect(put_list[:]), leads[j][:])
+            cc_wins.append(user_scores(j, j))
+
+        gw = keep.tile([P, PACK, SLOTS], BF16, name="gw")
+        c_got = keep.tile([P, PACK - 1, SLOTS], F32, name="c_got", tag="a_win")
+        for j in range(PACK - 1):
+            g = keep.tile([P, SLOTS], F32, name="g", tag="g", bufs=2)
+            nc.scalar.activation(c_got[:, j, :], cc_wins[j][:].indirect(user_list[:]), COPY)
+            if j == 0:
+                for h in range(2):
+                    nc.gpsimd.tensor_tensor(half(g, h), c_got[:, j, h * HALF:(h + 1) * HALF], lead0[h][:], SUB)
+            else:
+                nc.gpsimd.tensor_tensor(g[:], c_got[:, j, :], leads[j][:], SUB)
+            nc.gpsimd.tensor_scalar(gw[:, j, :], g[:], rowf_c[:, j:j + 1], 0.0, MULT, ADD)
+
+        j = PACK - 1
+        g_last = keep.tile([P, SLOTS], F32, name="g_last")
+        c_last = keep.tile([P, HALF], F32, name="c_last")
+        nc.scalar.activation(c_last[:], cc_wins[j][:].indirect(half_list(user_list, 1)), COPY)
+        nc.vector.tensor_tensor(half(g_last, 0), cc_wins[j][:].indirect(half_list(user_list, 0)), half(leads[j], 0), SUB)
+        nc.vector.tensor_tensor(half(g_last, 1), c_last[:], half(leads[j], 1), SUB)
+        nc.vector.tensor_scalar(gw[:, j, :], g_last[:], rowf_c[:, j:j + 1], None, MULT)
+
+        woven = [keep.tile([P, HALF, PACK], BF16, name="woven%d" % h, align_bytes=64) for h in range(2)]
+        for h in range(2):
+            src = gw[:, :, h * HALF:(h + 1) * HALF].rearrange("p j (c i) -> p c j i", i=4)
+            dst = woven[h][:].rearrange("p (c i) j -> p c j i", i=4)
+            if h == 0:
+                nc.vector.tensor_copy(dst, src)
+            else:
+                nc.scalar.copy(dst, src)
+        out_rows = out.rearrange("(u p) i -> p u i", p=P)
+        for h in range(2):
+            gw_codes = keep.tile([P, HALF], U32, name="gw_codes%d" % h, align_bytes=64)
+            gw_scales = keep.tile([P, HALF], U8, name="gw_scales%d" % h, align_bytes=64)
+            nc.vector.quantize_mx(
+                out=gw_codes[:].bitcast(FP8X4), scales=gw_scales[:], in_=woven[h][:].rearrange("p i j -> p (i j)"),
+            )
+            bank = psum.tile([P, 2, HALF], F32, name="y%d" % h, tag="bank0%d" % h)
+            for u in range(2):
+                nc.tensor.matmul_mx(
+                    out=bank[:, u, :], lhsT=fp4_cols(mix_w, u, P), lhsT_scale=mix_s[:, u * P:(u + 1) * P],
+                    rhs=gw_codes[:].bitcast(FP8X4), rhs_scale=gw_scales[:], start=True, stop=True,
+                )
+            y = keep.tile([P, 2, HALF], F32, name="y_sb%d" % h)
+            if h == 0:
+                nc.scalar.copy(y[:], bank[:])
+            else:
+                nc.vector.tensor_copy(y[:], bank[:])
+            nc.sync.dma_start(out=out_rows[:, :, h * HALF:(h + 1) * HALF], in_=y[:])

@@ -37,8 +37,8 @@ def tile_attend_tugged_threeq_mixed_kernel(
         keep = ctx.enter_context(tc.tile_pool(name="keep", bufs=1))
         psum = ctx.enter_context(tc.psum_pool(name="psum", bufs=1))
 
-        def load_query_half(src, h, name):
-            raw = keep.tile([P, PACK, Q // 2], F32, name=name)
+        def load_query_half(src, h, name, tag):
+            raw = keep.tile([P, PACK, Q // 2], F32, name=name, tag=tag)
             rows = src.rearrange("(p t) q -> p t q", t=PACK)
             nc.sync.dma_start(out=raw[:], in_=rows[:, :, h * (Q // 2):(h + 1) * (Q // 2)])
             return raw
@@ -65,21 +65,21 @@ def tile_attend_tugged_threeq_mixed_kernel(
             nc.sync.dma_start(out=col[:], in_=src.rearrange("(p j) o -> p (j o)", j=PACK))
             return col
 
-        q_raw0 = load_query_half(query, 0, "q_raw0")
-        q_raw1 = load_query_half(query, 1, "q_raw1")
+        q_raw0 = load_query_half(query, 0, "q_raw0", "q_raw0")
+        q_raw1 = load_query_half(query, 1, "q_raw1", "q_raw1")
         notes_s = load_scales(notes_scales, COLS, "notes_s")
         notes_w = load_fp4_words(notes_words, COLS, "notes_w")
+        note_list = load_list(offs2, "note_list")
         keys_w = keep.tile([P, COLS], U32, name="keys_w", align_bytes=64)
         nc.sync.dma_start(out=keys_w[:].bitcast(I32), in_=keys_words[0].rearrange("p n t -> p (n t)").bitcast(I32))
         keys_s = load_scales(keys_scales, COLS, "keys_s")
-        q2_raw0 = load_query_half(query2, 0, "q2_raw0")
-        q2_raw1 = load_query_half(query2, 1, "q2_raw1")
-        note_list = load_list(offs2, "note_list")
+        q2_raw0 = load_query_half(query2, 0, "q2_raw0", "a_win")
         token_list = load_list(offs, "token_list")
         put_list = load_list(offs3, "put_list")
+        q2_raw1 = load_query_half(query2, 1, "q2_raw1", "q2_raw1")
         users_w = load_fp4_words(users_words, COLS, "users_w")
-        users_s = load_scales(users_scales, COLS, "users_s")
         lam_c = load_row_factor(lam, "lam_c")
+        users_s = load_scales(users_scales, COLS, "users_s")
         user_list = load_list(offs4, "user_list")
         rowf_c = load_row_factor(rowf, "rowf_c")
         mix_w = load_fp4_words(mix_words, E, "mix_w")
@@ -107,8 +107,8 @@ def tile_attend_tugged_threeq_mixed_kernel(
             )
 
         q2_bf = keep.tile([P, PACK, P, PACK], BF16, name="q2_bf", tag="q2_bf", align_bytes=64)
-        nc.gpsimd.tensor_scalar(dealt(q2_bf, 0), as_loaded(q2_raw0), 1.0, 0.0, MULT, ADD)
-        nc.gpsimd.tensor_scalar(dealt(q2_bf, 1), as_loaded(q2_raw1), 1.0, 0.0, MULT, ADD)
+        nc.scalar.copy(dealt(q2_bf, 0), as_loaded(q2_raw0))
+        nc.vector.tensor_copy(dealt(q2_bf, 1), as_loaded(q2_raw1))
         q2_codes = keep.tile([P, Q], U32, name="q2_codes", align_bytes=64)
         q2_scales = keep.tile([P, Q], U8, name="q2_scales", align_bytes=64)
 
@@ -179,16 +179,15 @@ def tile_attend_tugged_threeq_mixed_kernel(
             nc.vector.tensor_copy(f1[:].indirect(half_list(put_list, h)), part[:])
             lead0.append(part)
 
-        leads = [None, lead_of(1, note_scores(1, 2), 0), lead_of(2, note_scores(2, 1), 2)]
-        b_win3 = note_scores(3, 0)
-        cc_wins = [user_scores(0, 3)]
-        leads.append(lead_of(3, b_win3, 3))
+        leads = [None, lead_of(1, note_scores(1, 1), 0), lead_of(2, note_scores(2, 0), 1)]
+        cc_wins = [user_scores(0, 2)]
+        leads.append(lead_of(3, note_scores(3, 2), 3))
         for j in range(1, PACK):
             nc.vector.tensor_copy(f1[:].indirect(put_list[:]), leads[j][:])
-            cc_wins.append(user_scores(j, j))
+            cc_wins.append(user_scores(j, j - 1))
 
         gw = keep.tile([P, PACK, SLOTS], BF16, name="gw")
-        c_got = keep.tile([P, PACK - 1, SLOTS], F32, name="c_got", tag="a_win")
+        c_got = keep.tile([P, PACK - 1, SLOTS], F32, name="c_got")
         for j in range(PACK - 1):
             g = keep.tile([P, SLOTS], F32, name="g", tag="g", bufs=2)
             nc.scalar.activation(c_got[:, j, :], cc_wins[j][:].indirect(user_list[:]), COPY)
@@ -197,24 +196,26 @@ def tile_attend_tugged_threeq_mixed_kernel(
                     nc.gpsimd.tensor_tensor(half(g, h), c_got[:, j, h * HALF:(h + 1) * HALF], lead0[h][:], SUB)
             else:
                 nc.gpsimd.tensor_tensor(g[:], c_got[:, j, :], leads[j][:], SUB)
-            nc.gpsimd.tensor_scalar(gw[:, j, :], g[:], rowf_c[:, j:j + 1], 0.0, MULT, ADD)
+            nc.scalar.activation(gw[:, j, :], g[:], COPY, scale=rowf_c[:, j:j + 1])
 
         j = PACK - 1
+        woven = [keep.tile([P, HALF, PACK], BF16, name="woven%d" % h, align_bytes=64) for h in range(2)]
+
+        def weave(copy, h, planes):
+            copy(woven[h][:, :, planes], gw[:, planes, h * HALF:(h + 1) * HALF].rearrange("p j i -> p i j"))
+
+        for h in range(2):
+            weave(nc.scalar.copy, h, slice(0, 2))
         g_last = keep.tile([P, SLOTS], F32, name="g_last")
         c_last = keep.tile([P, HALF], F32, name="c_last")
         nc.scalar.activation(c_last[:], cc_wins[j][:].indirect(half_list(user_list, 1)), COPY)
         nc.vector.tensor_tensor(half(g_last, 0), cc_wins[j][:].indirect(half_list(user_list, 0)), half(leads[j], 0), SUB)
         nc.vector.tensor_tensor(half(g_last, 1), c_last[:], half(leads[j], 1), SUB)
-        nc.vector.tensor_scalar(gw[:, j, :], g_last[:], rowf_c[:, j:j + 1], None, MULT)
-
-        woven = [keep.tile([P, HALF, PACK], BF16, name="woven%d" % h, align_bytes=64) for h in range(2)]
         for h in range(2):
-            src = gw[:, :, h * HALF:(h + 1) * HALF].rearrange("p j (c i) -> p c j i", i=4)
-            dst = woven[h][:].rearrange("p (c i) j -> p c j i", i=4)
-            if h == 0:
-                nc.vector.tensor_copy(dst, src)
-            else:
-                nc.scalar.copy(dst, src)
+            nc.vector.tensor_scalar(gw[:, j, h * HALF:(h + 1) * HALF], half(g_last, h), rowf_c[:, j:j + 1], None, MULT)
+        for h in range(2):
+            weave(nc.vector.tensor_copy, h, slice(2, 4))
+
         out_rows = out.rearrange("(u p) i -> p u i", p=P)
         for h in range(2):
             gw_codes = keep.tile([P, HALF], U32, name="gw_codes%d" % h, align_bytes=64)
@@ -222,15 +223,12 @@ def tile_attend_tugged_threeq_mixed_kernel(
             nc.vector.quantize_mx(
                 out=gw_codes[:].bitcast(FP8X4), scales=gw_scales[:], in_=woven[h][:].rearrange("p i j -> p (i j)"),
             )
-            bank = psum.tile([P, 2, HALF], F32, name="y%d" % h, tag="bank0%d" % h)
-            for u in range(2):
+            y = keep.tile([P, 2, HALF], F32, name="y_sb%d" % h)
+            for u, copy in enumerate((nc.scalar.copy, nc.vector.tensor_copy if h == 1 else nc.scalar.copy)):
+                bank = psum.tile([P, HALF], F32, name="y%d%d" % (h, u), tag="bank%d%d" % (h, u))
                 nc.tensor.matmul_mx(
-                    out=bank[:, u, :], lhsT=fp4_cols(mix_w, u, P), lhsT_scale=mix_s[:, u * P:(u + 1) * P],
+                    out=bank[:], lhsT=fp4_cols(mix_w, u, P), lhsT_scale=mix_s[:, u * P:(u + 1) * P],
                     rhs=gw_codes[:].bitcast(FP8X4), rhs_scale=gw_scales[:], start=True, stop=True,
                 )
-            y = keep.tile([P, 2, HALF], F32, name="y_sb%d" % h)
-            if h == 0:
-                nc.scalar.copy(y[:], bank[:])
-            else:
-                nc.vector.tensor_copy(y[:], bank[:])
+                copy(y[:, u, :], bank[:])
             nc.sync.dma_start(out=out_rows[:, :, h * HALF:(h + 1) * HALF], in_=y[:])

@@ -17,6 +17,8 @@ COPY = mybir.ActivationFunctionType.Copy
 
 P = 128
 PACK = 4
+LAST = PACK - 1
+D = 512
 Q = 512
 COLS = 1024
 SLOTS = 512
@@ -24,8 +26,10 @@ E = 256
 BANK = 512
 HALF = SLOTS // 2
 LIST_COLS = SLOTS // 16
+QUADRANT = 32
+SCALE_ROWS = 16
 
-FLOPS = 2 * 512 * 512 * 3 * 1024 + 2 * 512 * 256 * 512
+FLOPS = 2 * D * Q * 3 * COLS + 2 * Q * E * SLOTS
 
 
 def tile_attend_tugged_threeq_mixed_kernel(
@@ -47,7 +51,7 @@ def tile_attend_tugged_threeq_mixed_kernel(
             plane = keep.tile([P, width], U8, name=name, align_bytes=64)
             rows = src[0].bitcast(I32)
             for r in range(4):
-                nc.sync.dma_start(out=plane[r:P:32, :].bitcast(I32), in_=rows[r:16:4, :])
+                nc.sync.dma_start(out=plane[r:P:QUADRANT, :].bitcast(I32), in_=rows[r:SCALE_ROWS:4, :])
             return plane
 
         def load_fp4_words(src, width, name):
@@ -85,21 +89,24 @@ def tile_attend_tugged_threeq_mixed_kernel(
         mix_w = load_fp4_words(mix_words, E, "mix_w")
         mix_s = load_scales(mix_scales, E, "mix_s")
 
-        f1 = keep.tile([P, COLS], F32, name="f1")
-        nc.gpsimd.memset(f1[:], 0.0)
+        windows = [keep.tile([P, COLS], F32, name="f1_%d" % n) for n in range(2)]
+        for window in windows:
+            nc.gpsimd.memset(window[:], 0.0)
+        f1 = [windows[0], windows[0], windows[1], windows[0]]
 
-        def dealt(tile, h):
-            return tile[:, :, h * 64:(h + 1) * 64, :].rearrange("p j m t -> p m t j")
-
-        def as_loaded(raw):
-            return raw[:].rearrange("p t (m j) -> p m t j", j=PACK)
+        def deal(copy, tile, raw, h, j0, j1):
+            copy(
+                tile[:, j0:j1, h * (P // 2):(h + 1) * (P // 2), :].rearrange("p j m t -> p m j t"),
+                raw[:].rearrange("p t (m j) -> p m j t", j=PACK)[:, :, j0:j1, :],
+            )
 
         q_bf = keep.tile([P, PACK, P, PACK], BF16, name="q_bf", align_bytes=64)
-        nc.scalar.copy(dealt(q_bf, 0), as_loaded(q_raw0))
-        nc.vector.tensor_copy(dealt(q_bf, 1), as_loaded(q_raw1))
+        for j0, j1 in ((0, 1), (1, PACK)):
+            deal(nc.scalar.copy, q_bf, q_raw0, 0, j0, j1)
+            deal(nc.vector.tensor_copy, q_bf, q_raw1, 1, j0, j1)
         q_codes = keep.tile([P, Q], U32, name="q_codes", align_bytes=64)
         q_scales = keep.tile([P, Q], U8, name="q_scales", align_bytes=64)
-        for j0, j1 in ((0, 1), (1, 2), (2, 4)):
+        for j0, j1 in ((0, 1), (1, 2), (2, PACK)):
             nc.vector.quantize_mx(
                 out=q_codes[:, j0 * P:j1 * P].bitcast(FP8X4),
                 scales=q_scales[:, j0 * P:j1 * P],
@@ -107,8 +114,8 @@ def tile_attend_tugged_threeq_mixed_kernel(
             )
 
         q2_bf = keep.tile([P, PACK, P, PACK], BF16, name="q2_bf", tag="q2_bf", align_bytes=64)
-        nc.scalar.copy(dealt(q2_bf, 0), as_loaded(q2_raw0))
-        nc.vector.tensor_copy(dealt(q2_bf, 1), as_loaded(q2_raw1))
+        deal(nc.scalar.copy, q2_bf, q2_raw0, 0, 0, PACK)
+        deal(nc.vector.tensor_copy, q2_bf, q2_raw1, 1, 0, PACK)
         q2_codes = keep.tile([P, Q], U32, name="q2_codes", align_bytes=64)
         q2_scales = keep.tile([P, Q], U8, name="q2_scales", align_bytes=64)
 
@@ -157,7 +164,7 @@ def tile_attend_tugged_threeq_mixed_kernel(
             for n in range(2):
                 bank = score(q2_codes, q2_scales, j, fp4_cols(users_w, n, BANK), users_s, pair, n)
                 cols = slice(n * BANK, (n + 1) * BANK)
-                nc.vector.scalar_tensor_tensor(cc_win[:, cols], f1[:, cols], lam_c[:, j:j + 1], bank[:], MULT, ADD)
+                nc.vector.scalar_tensor_tensor(cc_win[:, cols], f1[j][:, cols], lam_c[:, j:j + 1], bank[:], MULT, ADD)
             return cc_win
 
         b_win0 = note_scores(0, 0)
@@ -166,69 +173,79 @@ def tile_attend_tugged_threeq_mixed_kernel(
         b_got0 = keep.tile([P, SLOTS], F32, name="b_got", tag="b_got", bufs=2)
         for h in range(2):
             nc.scalar.activation(half(b_got0, h), b_win0[:].indirect(half_list(note_list, h)), COPY)
-        lead0 = []
-        for h in range(2):
-            if h == 0:
-                part = keep.tile([P, HALF], F32, name="lead0_first")
-            else:
-                nc.vector.quantize_mx(
-                    out=q2_codes[:].bitcast(FP8X4), scales=q2_scales[:], in_=q2_bf[:].rearrange("p j m t -> p (j m t)"),
-                )
-                part = keep.tile([P, HALF], F32, name="lead0_second", tag="q2_bf", align_bytes=64)
-            nc.vector.tensor_tensor(part[:], a_win0[:].indirect(half_list(token_list, h)), half(b_got0, h), SUB)
-            nc.vector.tensor_copy(f1[:].indirect(half_list(put_list, h)), part[:])
-            lead0.append(part)
 
-        leads = [None, lead_of(1, note_scores(1, 1), 0), lead_of(2, note_scores(2, 0), 1)]
-        cc_wins = [user_scores(0, 2)]
-        leads.append(lead_of(3, note_scores(3, 2), 3))
-        for j in range(1, PACK):
-            nc.vector.tensor_copy(f1[:].indirect(put_list[:]), leads[j][:])
-            cc_wins.append(user_scores(j, j - 1))
+        def lead0_half(h, part):
+            nc.vector.tensor_tensor(part[:], a_win0[:].indirect(half_list(token_list, h)), half(b_got0, h), SUB)
+            nc.vector.tensor_copy(f1[0][:].indirect(half_list(put_list, h)), part[:])
+            return part
+
+        lead0 = [lead0_half(0, keep.tile([P, HALF], F32, name="lead0_first"))]
+        nc.vector.quantize_mx(
+            out=q2_codes[:].bitcast(FP8X4), scales=q2_scales[:], in_=q2_bf[:].rearrange("p j m t -> p (j m t)"),
+        )
+        lead0.append(lead0_half(1, keep.tile([P, HALF], F32, name="lead0_second", tag="q2_bf", align_bytes=64)))
 
         gw = keep.tile([P, PACK, SLOTS], BF16, name="gw")
-        c_got = keep.tile([P, PACK - 1, SLOTS], F32, name="c_got")
-        for j in range(PACK - 1):
-            g = keep.tile([P, SLOTS], F32, name="g", tag="g", bufs=2)
+
+        def put(j):
+            nc.vector.tensor_copy(f1[j][:].indirect(put_list[:]), leads[j][:])
+
+        def result_of(j):
+            g = keep.tile([P, SLOTS], F32, name="g%d" % j)
             nc.scalar.activation(c_got[:, j, :], cc_wins[j][:].indirect(user_list[:]), COPY)
             if j == 0:
                 for h in range(2):
-                    nc.gpsimd.tensor_tensor(half(g, h), c_got[:, j, h * HALF:(h + 1) * HALF], lead0[h][:], SUB)
+                    nc.gpsimd.tensor_tensor(half(g, h), half(c_got[:, j, :], h), lead0[h][:], SUB)
             else:
                 nc.gpsimd.tensor_tensor(g[:], c_got[:, j, :], leads[j][:], SUB)
-            nc.scalar.activation(gw[:, j, :], g[:], COPY, scale=rowf_c[:, j:j + 1])
+            nc.gpsimd.tensor_scalar(gw[:, j, :], g[:], rowf_c[:, j:j + 1], 0.0, MULT, ADD)
 
-        j = PACK - 1
-        woven = [keep.tile([P, HALF, PACK], BF16, name="woven%d" % h, align_bytes=64) for h in range(2)]
+        leads = [None, lead_of(1, note_scores(1, 1), 0), lead_of(2, note_scores(2, 0), 1)]
+        cc_wins = [user_scores(0, 2)]
+        leads.append(lead_of(LAST, note_scores(LAST, 2), 3))
+        c_got = keep.tile([P, LAST, SLOTS], F32, name="c_all", tag="a_win")
+        for j in range(1, LAST):
+            put(j)
+            cc_wins.append(user_scores(j, j - 1))
+        result_of(0)
+        put(LAST)
+        for j in range(1, LAST):
+            result_of(j)
+        cc_wins.append(user_scores(LAST, 2))
 
-        def weave(copy, h, planes):
-            copy(woven[h][:, :, planes], gw[:, planes, h * HALF:(h + 1) * HALF].rearrange("p j i -> p i j"))
+        woven = [keep.tile([P, HALF, PACK], BF16, name="woven%d" % (h * HALF), align_bytes=64) for h in range(2)]
+
+        def weave(copy, h, places):
+            copy(woven[h][:, :, places], gw[:, places, h * HALF:(h + 1) * HALF].rearrange("p j i -> p i j"))
 
         for h in range(2):
             weave(nc.scalar.copy, h, slice(0, 2))
         g_last = keep.tile([P, SLOTS], F32, name="g_last")
         c_last = keep.tile([P, HALF], F32, name="c_last")
-        nc.scalar.activation(c_last[:], cc_wins[j][:].indirect(half_list(user_list, 1)), COPY)
-        nc.vector.tensor_tensor(half(g_last, 0), cc_wins[j][:].indirect(half_list(user_list, 0)), half(leads[j], 0), SUB)
-        nc.vector.tensor_tensor(half(g_last, 1), c_last[:], half(leads[j], 1), SUB)
+        nc.scalar.activation(c_last[:], cc_wins[LAST][:].indirect(half_list(user_list, 1)), COPY)
+        nc.vector.tensor_tensor(
+            half(g_last, 0), cc_wins[LAST][:].indirect(half_list(user_list, 0)), half(leads[LAST], 0), SUB,
+        )
+        nc.vector.tensor_tensor(half(g_last, 1), c_last[:], half(leads[LAST], 1), SUB)
         for h in range(2):
-            nc.vector.tensor_scalar(gw[:, j, h * HALF:(h + 1) * HALF], half(g_last, h), rowf_c[:, j:j + 1], None, MULT)
+            nc.vector.tensor_scalar(half(gw[:, LAST, :], h), half(g_last, h), rowf_c[:, LAST:PACK], None, MULT)
         for h in range(2):
-            weave(nc.vector.tensor_copy, h, slice(2, 4))
+            weave(nc.vector.tensor_copy, h, slice(2, PACK))
 
         out_rows = out.rearrange("(u p) i -> p u i", p=P)
+        emptied_by = ((nc.scalar.copy, nc.scalar.copy), (nc.scalar.copy, nc.vector.tensor_copy))
         for h in range(2):
             gw_codes = keep.tile([P, HALF], U32, name="gw_codes%d" % h, align_bytes=64)
             gw_scales = keep.tile([P, HALF], U8, name="gw_scales%d" % h, align_bytes=64)
             nc.vector.quantize_mx(
                 out=gw_codes[:].bitcast(FP8X4), scales=gw_scales[:], in_=woven[h][:].rearrange("p i j -> p (i j)"),
             )
-            y = keep.tile([P, 2, HALF], F32, name="y_sb%d" % h)
-            for u, copy in enumerate((nc.scalar.copy, nc.vector.tensor_copy if h == 1 else nc.scalar.copy)):
+            y = keep.tile([P, E // P, HALF], F32, name="y_sb%d" % h)
+            for u in range(E // P):
                 bank = psum.tile([P, HALF], F32, name="y%d%d" % (h, u), tag="bank%d%d" % (h, u))
                 nc.tensor.matmul_mx(
                     out=bank[:], lhsT=fp4_cols(mix_w, u, P), lhsT_scale=mix_s[:, u * P:(u + 1) * P],
                     rhs=gw_codes[:].bitcast(FP8X4), rhs_scale=gw_scales[:], start=True, stop=True,
                 )
-                copy(y[:, u, :], bank[:])
+                emptied_by[h][u](y[:, u, :], bank[:])
             nc.sync.dma_start(out=out_rows[:, :, h * HALF:(h + 1) * HALF], in_=y[:])

from contextlib import ExitStack

import concourse.mybir as mybir

F32 = mybir.dt.float32
BF16 = mybir.dt.bfloat16
I32 = mybir.dt.int32
U32 = mybir.dt.uint32
U16 = mybir.dt.uint16
U8 = mybir.dt.uint8
FP8X4 = mybir.dt.float8_e4m3fn_x4
FP4X4 = mybir.dt.float4_e2m1fn_x4
MULT = mybir.AluOpType.mult
ADD = mybir.AluOpType.add
SUB = mybir.AluOpType.subtract
COPY = mybir.ActivationFunctionType.Copy

P = 128
PACK = 4
LAST = PACK - 1
D = 512
Q = 512
COLS = 1024
SLOTS = 512
E = 256
BANK = 512
HALF = SLOTS // 2
LIST_COLS = SLOTS // 16
QUADRANT = 32
SCALE_ROWS = 16

FLOPS = 2 * D * Q * 3 * COLS + 2 * Q * E * SLOTS


def tile_attend_tugged_threeq_mixed_kernel(
    tc, query, query2, keys_words, keys_scales, notes_words, notes_scales, users_words, users_scales,
    lam, rowf, mix_words, mix_scales, offs, offs2, offs3, offs4, out,
):
    nc = tc.nc
    with ExitStack() as ctx:
        keep = ctx.enter_context(tc.tile_pool(name="keep", bufs=1))
        psum = ctx.enter_context(tc.psum_pool(name="psum", bufs=1))

        def load_query_half(src, h, name, tag):
            raw = keep.tile([P, PACK, Q // 2], F32, name=name, tag=tag)
            rows = src.rearrange("(p t) q -> p t q", t=PACK)
            nc.sync.dma_start(out=raw[:], in_=rows[:, :, h * (Q // 2):(h + 1) * (Q // 2)])
            return raw

        def load_scales(src, width, name):
            plane = keep.tile([P, width], U8, name=name, align_bytes=64)
            rows = src[0].bitcast(I32)
            for r in range(4):
                nc.sync.dma_start(out=plane[r:P:QUADRANT, :].bitcast(I32), in_=rows[r:SCALE_ROWS:4, :])
            return plane

        def load_fp4_words(src, width, name):
            words = keep.tile([P, 2 * width], U8, name=name, align_bytes=64)
            nc.sync.dma_start(out=words[:].bitcast(I32), in_=src[0].bitcast(I32))
            return words

        def load_list(src, name):
            lst = keep.tile([P, LIST_COLS], U16, name=name)
            nc.sync.dma_start(out=lst[:], in_=src)
            return lst

        def load_row_factor(src, name):
            col = keep.tile([P, PACK], F32, name=name)
            nc.sync.dma_start(out=col[:], in_=src.rearrange("(p j) o -> p (j o)", j=PACK))
            return col

        q_raw0 = load_query_half(query, 0, "q_raw0", "q_raw0")
        q_raw1 = load_query_half(query, 1, "q_raw1", "q_raw1")
        notes_s = load_scales(notes_scales, COLS, "notes_s")
        notes_w = load_fp4_words(notes_words, COLS, "notes_w")
        note_list = load_list(offs2, "note_list")
        keys_w = keep.tile([P, COLS], U32, name="keys_w", align_bytes=64)
        nc.sync.dma_start(out=keys_w[:].bitcast(I32), in_=keys_words[0].rearrange("p n t -> p (n t)").bitcast(I32))
        keys_s = load_scales(keys_scales, COLS, "keys_s")
        q2_raw0 = load_query_half(query2, 0, "q2_raw0", "a_win")
        token_list = load_list(offs, "token_list")
        put_list = load_list(offs3, "put_list")
        q2_raw1 = load_query_half(query2, 1, "q2_raw1", "q2_raw1")
        users_w = load_fp4_words(users_words, COLS, "users_w")
        lam_c = load_row_factor(lam, "lam_c")
        users_s = load_scales(users_scales, COLS, "users_s")
        user_list = load_list(offs4, "user_list")
        rowf_c = load_row_factor(rowf, "rowf_c")
        mix_w = load_fp4_words(mix_words, E, "mix_w")
        mix_s = load_scales(mix_scales, E, "mix_s")

        windows = [keep.tile([P, COLS], F32, name="f1_%d" % n) for n in range(2)]
        for window in windows:
            nc.gpsimd.memset(window[:], 0.0)
        f1 = [windows[0], windows[0], windows[1], windows[0]]

        def deal(copy, tile, raw, h, j0, j1):
            copy(
                tile[:, j0:j1, h * (P // 2):(h + 1) * (P // 2), :].rearrange("p j m t -> p m j t"),
                raw[:].rearrange("p t (m j) -> p m j t", j=PACK)[:, :, j0:j1, :],
            )

        q_bf = keep.tile([P, PACK, P, PACK], BF16, name="q_bf", align_bytes=64)
        for j0, j1 in ((0, 1), (1, PACK)):
            deal(nc.scalar.copy, q_bf, q_raw0, 0, j0, j1)
            deal(nc.vector.tensor_copy, q_bf, q_raw1, 1, j0, j1)
        q_codes = keep.tile([P, Q], U32, name="q_codes", align_bytes=64)
        q_scales = keep.tile([P, Q], U8, name="q_scales", align_bytes=64)
        for j0, j1 in ((0, 1), (1, 2), (2, PACK)):
            nc.vector.quantize_mx(
                out=q_codes[:, j0 * P:j1 * P].bitcast(FP8X4),
                scales=q_scales[:, j0 * P:j1 * P],
                in_=q_bf[:, j0:j1, :, :].rearrange("p j m t -> p (j m t)"),
            )

        q2_bf = keep.tile([P, PACK, P, PACK], BF16, name="q2_bf", tag="q2_bf", align_bytes=64)
        deal(nc.scalar.copy, q2_bf, q2_raw0, 0, 0, PACK)
        deal(nc.vector.tensor_copy, q2_bf, q2_raw1, 1, 0, PACK)
        q2_codes = keep.tile([P, Q], U32, name="q2_codes", align_bytes=64)
        q2_scales = keep.tile([P, Q], U8, name="q2_scales", align_bytes=64)

        def score(codes, scales, j, moving, moving_scales, pair, n):
            bank = psum.tile([P, BANK], F32, name="bank%d%d" % (pair, n), tag="bank%d%d" % (pair, n))
            nc.tensor.matmul_mx(
                out=bank[:], lhsT=codes[:, j * P:(j + 1) * P].bitcast(FP8X4), lhsT_scale=scales[:, j * P:(j + 1) * P],
                rhs=moving, rhs_scale=moving_scales[:, n * BANK:(n + 1) * BANK], start=True, stop=True,
            )
            return bank

        def fp4_cols(words, n, width):
            return words[:, 2 * n * width:2 * (n + 1) * width].bitcast(FP4X4)

        def half_list(lst, h):
            return lst[:, h * (LIST_COLS // 2):(h + 1) * (LIST_COLS // 2)]

        def half(tile, h):
            return tile[:, h * HALF:(h + 1) * HALF]

        def note_scores(j, pair):
            win = keep.tile([P, COLS], F32, name="b_win", tag="b_win", bufs=2)
            for n in range(2):
                bank = score(q_codes, q_scales, j, fp4_cols(notes_w, n, BANK), notes_s, pair, n)
                nc.scalar.copy(win[:, n * BANK:(n + 1) * BANK], bank[:])
            return win

        def token_scores(j, pair, win, copy):
            for n in range(2):
                bank = score(q_codes, q_scales, j, keys_w[:, n * BANK:(n + 1) * BANK].bitcast(FP8X4), keys_s, pair, n)
                copy(win[:, n * BANK:(n + 1) * BANK], bank[:])

        def lead_of(j, b_win, a_pair):
            a_win = keep.tile([P, COLS], F32, name="a_win", tag="a_win")
            token_scores(j, a_pair, a_win, nc.scalar.copy)
            b_got = keep.tile([P, SLOTS], F32, name="b_got", tag="b_got", bufs=2)
            a_got = keep.tile([P, SLOTS], F32, name="a_got", tag="a_got", bufs=2)
            lead = keep.tile([P, SLOTS], F32, name="lead%d" % j)
            nc.scalar.activation(b_got[:], b_win[:].indirect(note_list[:]), COPY)
            nc.scalar.activation(a_got[:], a_win[:].indirect(token_list[:]), COPY)
            nc.gpsimd.tensor_tensor(lead[:], a_got[:], b_got[:], SUB)
            return lead

        def user_scores(j, pair):
            cc_win = keep.tile([P, COLS], F32, name="cc%d" % j)
            for n in range(2):
                bank = score(q2_codes, q2_scales, j, fp4_cols(users_w, n, BANK), users_s, pair, n)
                cols = slice(n * BANK, (n + 1) * BANK)
                nc.vector.scalar_tensor_tensor(cc_win[:, cols], f1[j][:, cols], lam_c[:, j:j + 1], bank[:], MULT, ADD)
            return cc_win

        b_win0 = note_scores(0, 0)
        a_win0 = keep.tile([P, COLS], F32, name="a_win0")
        token_scores(0, 1, a_win0, nc.vector.tensor_copy)
        b_got0 = keep.tile([P, SLOTS], F32, name="b_got", tag="b_got", bufs=2)
        for h in range(2):
            nc.scalar.activation(half(b_got0, h), b_win0[:].indirect(half_list(note_list, h)), COPY)

        def lead0_half(h, part):
            nc.vector.tensor_tensor(part[:], a_win0[:].indirect(half_list(token_list, h)), half(b_got0, h), SUB)
            nc.vector.tensor_copy(f1[0][:].indirect(half_list(put_list, h)), part[:])
            return part

        lead0 = [lead0_half(0, keep.tile([P, HALF], F32, name="lead0_first"))]
        nc.vector.quantize_mx(
            out=q2_codes[:].bitcast(FP8X4), scales=q2_scales[:], in_=q2_bf[:].rearrange("p j m t -> p (j m t)"),
        )
        lead0.append(lead0_half(1, keep.tile([P, HALF], F32, name="lead0_second", tag="q2_bf", align_bytes=64)))

        gw = keep.tile([P, PACK, SLOTS], BF16, name="gw")

        def put(j):
            nc.vector.tensor_copy(f1[j][:].indirect(put_list[:]), leads[j][:])

        def result_of(j):
            g = keep.tile([P, SLOTS], F32, name="g%d" % j)
            nc.scalar.activation(c_got[:, j, :], cc_wins[j][:].indirect(user_list[:]), COPY)
            if j == 0:
                for h in range(2):
                    nc.gpsimd.tensor_tensor(half(g, h), half(c_got[:, j, :], h), lead0[h][:], SUB)
            else:
                nc.gpsimd.tensor_tensor(g[:], c_got[:, j, :], leads[j][:], SUB)
            nc.gpsimd.tensor_scalar(gw[:, j, :], g[:], rowf_c[:, j:j + 1], 0.0, MULT, ADD)

        leads = [None, lead_of(1, note_scores(1, 1), 0), lead_of(2, note_scores(2, 0), 1)]
        cc_wins = [user_scores(0, 2)]
        leads.append(lead_of(LAST, note_scores(LAST, 2), 3))
        c_got = keep.tile([P, LAST, SLOTS], F32, name="c_all", tag="a_win")
        for j in range(1, LAST):
            put(j)
            cc_wins.append(user_scores(j, j - 1))
        result_of(0)
        put(LAST)
        for j in range(1, LAST):
            result_of(j)
        cc_wins.append(user_scores(LAST, 2))

        woven = [keep.tile([P, HALF, PACK], BF16, name="woven%d" % (h * HALF), align_bytes=64) for h in range(2)]

        def weave(copy, h, places):
            copy(woven[h][:, :, places], gw[:, places, h * HALF:(h + 1) * HALF].rearrange("p j i -> p i j"))

        for h in range(2):
            weave(nc.scalar.copy, h, slice(0, 2))
        g_last = keep.tile([P, SLOTS], F32, name="g_last")
        c_last = keep.tile([P, HALF], F32, name="c_last")
        nc.scalar.activation(c_last[:], cc_wins[LAST][:].indirect(half_list(user_list, 1)), COPY)
        nc.vector.tensor_tensor(
            half(g_last, 0), cc_wins[LAST][:].indirect(half_list(user_list, 0)), half(leads[LAST], 0), SUB,
        )
        nc.vector.tensor_tensor(half(g_last, 1), c_last[:], half(leads[LAST], 1), SUB)
        for h in range(2):
            nc.vector.tensor_scalar(half(gw[:, LAST, :], h), half(g_last, h), rowf_c[:, LAST:PACK], None, MULT)
        for h in range(2):
            weave(nc.vector.tensor_copy, h, slice(2, PACK))

        out_rows = out.rearrange("(u p) i -> p u i", p=P)
        emptied_by = ((nc.scalar.copy, nc.scalar.copy), (nc.scalar.copy, nc.vector.tensor_copy))
        for h in range(2):
            gw_codes = keep.tile([P, HALF], U32, name="gw_codes%d" % h, align_bytes=64)
            gw_scales = keep.tile([P, HALF], U8, name="gw_scales%d" % h, align_bytes=64)
            nc.vector.quantize_mx(
                out=gw_codes[:].bitcast(FP8X4), scales=gw_scales[:], in_=woven[h][:].rearrange("p i j -> p (i j)"),
            )
            y = keep.tile([P, E // P, HALF], F32, name="y_sb%d" % h)
            for u in range(E // P):
                bank = psum.tile([P, HALF], F32, name="y%d%d" % (h, u), tag="bank%d%d" % (h, u))
                nc.tensor.matmul_mx(
                    out=bank[:], lhsT=fp4_cols(mix_w, u, P), lhsT_scale=mix_s[:, u * P:(u + 1) * P],
                    rhs=gw_codes[:].bitcast(FP8X4), rhs_scale=gw_scales[:], start=True, stop=True,
                )
                emptied_by[h][u](y[:, u, :], bank[:])
            nc.sync.dma_start(out=out_rows[:, :, h * HALF:(h + 1) * HALF], in_=y[:])
